import numpy as np
import ml_dtypes


def mxq(x, axis, fmt="e4m3"):
    dtype, down = {"e4m3": (ml_dtypes.float8_e4m3fn, 7), "e5m2": (ml_dtypes.float8_e5m2, 14)}[fmt]
    v = np.moveaxis(np.asarray(x, np.float32).astype(ml_dtypes.bfloat16).astype(np.float64), axis, -1)
    blocks = v.reshape(v.shape[:-1] + (-1, 32))
    amax = np.abs(blocks).max(-1, keepdims=True)
    byte = np.maximum(np.where(amax > 0, np.frexp(amax)[1] - 1 + 127, 0) - down, 1)
    scale = np.exp2(byte - 127.0)
    codes = (blocks / scale).astype(np.float32).astype(dtype).astype(np.float64)
    return np.moveaxis((codes * scale).reshape(v.shape), -1, axis)


WIDE = False


def mx_kscale(k):
    if not WIDE:
        return np.ones(k)
    levels = np.array([10, -10, 5, -5, 0])
    if k % 512:
        return np.exp2(np.random.permutation(np.resize(levels, k // 32))).repeat(32)
    a = np.empty((k // 512, 16))
    for p in range(k // 512):
        a[p, :8] = np.random.permutation(np.resize(levels, 8))
        for g in range(8):
            far = levels[np.abs(levels - a[p, g]) >= 10]
            a[p, g + 8] = far[np.random.randint(len(far))]
    return np.exp2(a.ravel()).repeat(32)


BF16 = ml_dtypes.bfloat16


def bf(x):
    return np.asarray(x, np.float32).astype(BF16)


def f64(x):
    return np.asarray(x).astype(np.float64)


E2M1 = np.array([0.0, 0.5, 1.0, 1.5, 2.0, 3.0, 4.0, 6.0, -0.0, -0.5, -1.0, -1.5, -2.0, -3.0, -4.0, -6.0])


def pack_weight(w, fmt):
    k, n = w.shape
    w = f64(bf(w)).reshape(k // 32, 32, n)
    amax = np.abs(w).max(1)
    if fmt == "e4m3":
        byte = np.frexp(amax)[1] - 1 + 127 - 7
    else:
        mant, ex = np.frexp(amax / 6.0)
        byte = np.where(mant > 0.5, ex, ex - 1) + 127
    byte = np.clip(np.where(amax > 0, byte, 1), 1, 254)
    scaled = (w * np.exp2(127.0 - byte)[:, None, :]).reshape(k, n).astype(np.float32)
    by_word = np.ascontiguousarray(scaled.reshape(k // 512, 128, 4, n).transpose(0, 1, 3, 2))
    if fmt == "e4m3":
        words = by_word.astype(ml_dtypes.float8_e4m3fn).view(np.uint8)
    else:
        c = by_word.astype(ml_dtypes.float4_e2m1fn).view(np.uint8) & 0xF
        words = c[..., 0::2] | (c[..., 1::2] << 4)
    return np.ascontiguousarray(words), np.ascontiguousarray(byte.astype(np.uint8).reshape(k // 512, 16, n))


def unpack_weight(words, scales, fmt):
    g, p, n, _ = words.shape
    if fmt == "e4m3":
        vals = np.ascontiguousarray(words).view(ml_dtypes.float8_e4m3fn).astype(np.float64)
    else:
        nib = np.empty((g, p, n, 4), np.uint8)
        nib[..., 0::2] = words & 0xF
        nib[..., 1::2] = words >> 4
        vals = E2M1[nib]
    vals = vals * np.repeat(np.exp2(scales.astype(np.float64) - 127.0), 8, axis=1)[..., None]
    return vals.transpose(0, 1, 3, 2).reshape(g * 512, n)
def pack4(w):
    words, scales = pack_weight(w, "e2m1")
    return words.reshape(words.shape[0], 128, -1), scales


def unpack4(words, scales):
    return unpack_weight(words.reshape(words.shape[0], 128, -1, 2), scales, "e2m1")


T, C, R = 2048, 1024, 512


def setup_inputs():
    s = mx_kscale(T)[:, None]
    e = np.exp(np.random.standard_normal((T, C)))
    gamma = e / e.sum(axis=1, keepdims=True) * C
    z1 = np.random.standard_normal((T, R)) / np.sqrt(T)
    z2 = np.random.standard_normal((T, R)) / np.sqrt(T)
    z3 = np.random.standard_normal((T, R)) / np.sqrt(T)
    z1_words, z1_scales = pack4(z1 / s)
    z2_words, z2_scales = pack_weight(z2 / s, "e4m3")
    return {"gamma": bf(gamma * s),
            "z1_words": z1_words, "z1_scales": z1_scales,
            "z2_words": z2_words, "z2_scales": z2_scales,
            "z3": bf(z3 / s),
            "loadings": bf(np.random.standard_normal((C, R)))}


def reference(gamma, z1_words, z1_scales, z2_words, z2_scales, z3, loadings):
    g = mxq(f64(gamma), 0, "e4m3").T
    b1 = g @ unpack4(z1_words, z1_scales)
    a = g @ unpack_weight(z2_words, z2_scales, "e4m3")
    b3 = g @ mxq(f64(z3), 0, "e4m3")
    shrink = 1 / (1 + np.exp(-a))
    return f64(loadings) * (shrink * (b1 + b3))

@@ -1,0 +1,180 @@
+from contextlib import ExitStack
+
+import concourse.mybir as mybir
+
+T, C, R = 2048, 1024, 512
+FLOPS = 3 * 2 * T * C * R
+
+F32 = mybir.dt.float32
+BF16 = mybir.dt.bfloat16
+I32 = mybir.dt.int32
+U32 = mybir.dt.uint32
+U8 = mybir.dt.uint8
+FP8X4 = mybir.dt.float8_e4m3fn_x4
+FP4X4 = mybir.dt.float4_e2m1fn_x4
+MULT = mybir.AluOpType.mult
+SIGMOID = mybir.ActivationFunctionType.Sigmoid
+
+P = 128
+PACK = 4
+K_PASS = P * PACK
+PASSES = T // K_PASS
+TILES = C // P
+CHUNK = 512
+HALF = CHUNK // 2
+QUARTER = CHUNK // 4
+NEIGHBOURS = 4
+QUADRANTS = 4
+
+
+def interleave_views(grouped, raw, c0, width):
+    dst = grouped[:].rearrange("p (c i t) -> p c t i", i=NEIGHBOURS, t=PACK)
+    src = raw[:, :, c0 : c0 + width].rearrange("p t (c i) -> p c t i", i=NEIGHBOURS)
+    return dst, src
+
+
+def tile_baum_welch_projection_s10_kernel(tc, gamma, z1_words, z1_scales, z2_words, z2_scales, z3, loadings, out):
+    nc = tc.nc
+    with ExitStack() as ctx:
+        keep = ctx.enter_context(tc.tile_pool(name="keep", bufs=1))
+        psum = ctx.enter_context(tc.psum_pool(name="psum", bufs=1))
+        ctx.enter_context(tc.manual_schedule())
+
+        z1s_first = keep.tile([P, R], U8, name="z1s_first", align_bytes=64)
+        z1s_rest = keep.tile([P, PASSES - 1, R], U8, name="z1s_rest", align_bytes=64)
+        z2s = keep.tile([P, R], U8, name="z2s", align_bytes=64)
+        nc.vector.memset(z1s_first[:].bitcast(I32), 0)
+        nc.vector.memset(z1s_rest[:].bitcast(I32), 0)
+        nc.vector.memset(z2s[:].bitcast(I32), 0)
+
+        raw = {}
+        z1w = {}
+
+        def load_chunk(key):
+            kind, g, h = key
+            src = gamma if kind == "gamma" else z3
+            rows = src[g * K_PASS : (g + 1) * K_PASS, h * CHUNK : (h + 1) * CHUNK]
+            raw[key] = keep.tile([P, PACK, CHUNK], BF16, name="raw_%s_%d_%d" % key)
+            nc.sync.dma_start(out=raw[key][:], in_=rows.rearrange("(p t) c -> p t c", t=PACK))
+
+        def load_z1_words(g):
+            z1w[g] = keep.tile([P, 2 * R], U8, name="z1w_%d" % g, align_bytes=64)
+            nc.sync.dma_start(out=z1w[g][:].bitcast(I32), in_=z1_words[g].bitcast(I32))
+
+        chunks = [("gamma", 0, 0), ("z3", 0, 0), ("gamma", 0, 1)]
+        for g in range(1, PASSES):
+            chunks.extend([("z3", g, 0), ("gamma", g, 0), ("gamma", g, 1)])
+
+        load_chunk(chunks[0])
+        for q in range(QUADRANTS):
+            nc.sync.dma_start(out=z1s_first[32 * q : 32 * q + 4, :].bitcast(I32), in_=z1_scales[0, 4 * q : 4 * q + 4, :].bitcast(I32))
+        load_z1_words(0)
+        load_chunk(chunks[1])
+        load_chunk(chunks[2])
+        for q in range(QUADRANTS):
+            nc.sync.dma_start(
+                out=z1s_rest[32 * q : 32 * q + 4, :, :].bitcast(I32),
+                in_=z1_scales[1:, 4 * q : 4 * q + 4, :].rearrange("g r n -> r g n").bitcast(I32),
+            )
+        for g in range(1, PASSES):
+            load_chunk(chunks[3 * g])
+            load_z1_words(g)
+            load_chunk(chunks[3 * g + 1])
+            load_chunk(chunks[3 * g + 2])
+
+        load_tiles = []
+
+        def load_loadings(h):
+            rows = loadings[h * CHUNK : (h + 1) * CHUNK, :]
+            tile = keep.tile([P, TILES // 2, R], BF16, name="loadings_%d" % h)
+            nc.sync.dma_start(out=tile[:], in_=rows.rearrange("(m p) r -> p m r", p=P))
+            load_tiles.append(tile)
+
+        load_loadings(0)
+        for q in range(QUADRANTS):
+            nc.sync.dma_start(out=z2s[32 * q : 32 * q + 16, :].bitcast(I32), in_=z2_scales[:, 4 * q : 4 * q + 4, :].bitcast(I32))
+        z2w = keep.tile([P, PASSES, R], U32, name="z2w", align_bytes=64)
+        nc.sync.dma_start(out=z2w[:].bitcast(I32), in_=z2_words.rearrange("g p n t -> p g (n t)").bitcast(I32))
+        load_loadings(1)
+
+        codes = {}
+        scales = {}
+
+        def quantize(key, grouped, c0, width):
+            nc.vector.quantize_mx(
+                out=codes[key][:, c0 : c0 + width].bitcast(FP8X4),
+                scales=scales[key][:, c0 : c0 + width],
+                in_=grouped[:],
+            )
+
+        pending = None
+        for key in chunks:
+            codes[key] = keep.tile([P, CHUNK], U32, name="codes_%s_%d_%d" % key, align_bytes=64)
+            scales[key] = keep.tile([P, CHUNK], U8, name="scales_%s_%d_%d" % key, align_bytes=64)
+            by_scalar = keep.tile([P, HALF * PACK], BF16, name="gs_%s_%d_%d" % key, align_bytes=64)
+            dst, src = interleave_views(by_scalar, raw[key], HALF, HALF)
+            nc.scalar.copy(out=dst, in_=src)
+            if pending is not None:
+                quantize(*pending)
+            by_vector = []
+            for j in range(2):
+                grouped = keep.tile([P, QUARTER * PACK], BF16, name="gv%d_%s_%d_%d" % ((j,) + key), align_bytes=64)
+                dst, src = interleave_views(grouped, raw[key], j * QUARTER, QUARTER)
+                nc.vector.tensor_copy(out=dst, in_=src)
+                by_vector.append(grouped)
+            for j in range(2):
+                quantize(key, by_vector[j], j * QUARTER, QUARTER)
+            pending = (key, by_scalar, HALF, HALF)
+        quantize(*pending)
+
+        def posteriors(m, g):
+            key = ("gamma", g, m // 4)
+            cols = slice((m % 4) * P, (m % 4 + 1) * P)
+            return codes[key][:, cols].bitcast(FP8X4), scales[key][:, cols]
+
+        b_acc = [psum.tile([P, R], F32, name="b_acc_%d" % m, tag="bank%d" % m) for m in range(TILES)]
+
+        def z1_pass(m, g, start, stop):
+            lhsT, lhsT_scale = posteriors(m, g)
+            plane = z1s_first[:] if g == 0 else z1s_rest[:, g - 1, :]
+            nc.tensor.matmul_mx(out=b_acc[m][:], lhsT=lhsT, lhsT_scale=lhsT_scale, rhs=z1w[g][:].bitcast(FP4X4), rhs_scale=plane, start=start, stop=stop)
+
+        def z3_pass(m, g, start, stop):
+            lhsT, lhsT_scale = posteriors(m, g)
+            key = ("z3", g, 0)
+            nc.tensor.matmul_mx(out=b_acc[m][:], lhsT=lhsT, lhsT_scale=lhsT_scale, rhs=codes[key][:].bitcast(FP8X4), rhs_scale=scales[key][:], start=start, stop=stop)
+
+        for m in range(TILES // 2):
+            z1_pass(m, 0, True, False)
+        for m in range(TILES // 2):
+            z3_pass(m, 0, False, False)
+        for m in range(TILES // 2, TILES):
+            z1_pass(m, 0, True, False)
+            z3_pass(m, 0, False, False)
+        for g in range(1, PASSES):
+            for m in range(TILES):
+                z1_pass(m, g, False, False)
+                z3_pass(m, g, False, g == PASSES - 1)
+
+        loaded = []
+        for m in range(TILES):
+            tile = keep.tile([P, R], F32, name="loaded_%d" % m)
+            nc.vector.tensor_tensor(out=tile[:], in0=b_acc[m][:], in1=load_tiles[m // 4][:, m % 4, :], op=MULT)
+            loaded.append(tile)
+
+        pieces = [(m, 0, R) for m in range(TILES - 1)] + [(TILES - 1, 0, HALF), (TILES - 1, HALF, HALF)]
+        for n, (m, c0, width) in enumerate(pieces):
+            cols = slice(c0, c0 + width)
+            a_acc = psum.tile([P, R], F32, name="a_acc_%d" % n, tag="bank%d" % (n % TILES))
+            for g in range(PASSES):
+                lhsT, lhsT_scale = posteriors(m, g)
+                nc.tensor.matmul_mx(
+                    out=a_acc[:, :width], lhsT=lhsT, lhsT_scale=lhsT_scale,
+                    rhs=z2w[:, g, cols].bitcast(FP8X4), rhs_scale=z2s[4 * g :, cols],
+                    start=(g == 0), stop=(g == PASSES - 1),
+                )
+            shrink = keep.tile([P, width], F32, name="shrink_%d" % n)
+            nc.scalar.activation(out=shrink[:], in_=a_acc[:, :width], func=SIGMOID)
+            result = keep.tile([P, width], F32, name="result_%d" % n)
+            nc.vector.tensor_tensor(out=result[:], in0=shrink[:], in1=loaded[m][:, cols], op=MULT)
+            nc.sync.dma_start(out=out[m * P : (m + 1) * P, cols], in_=result[:])

@@ -20,15 +20,18 @@ PACK = 4
 K_PASS = P * PACK
 PASSES = T // K_PASS
 TILES = C // P
-CHUNK = 512
-HALF = CHUNK // 2
-QUARTER = CHUNK // 4
+WIDE = 512
+NARROW = 256
 NEIGHBOURS = 4
 QUADRANTS = 4
+EARLY_TILES = 4
+LEAD = 4
+VECTOR_COLS = 112
+WARM = 16
 
 
 def interleave_views(grouped, raw, c0, width):
-    dst = grouped[:].rearrange("p (c i t) -> p c t i", i=NEIGHBOURS, t=PACK)
+    dst = grouped.rearrange("p (c i t) -> p c t i", i=NEIGHBOURS, t=PACK)
     src = raw[:, :, c0 : c0 + width].rearrange("p t (c i) -> p c t i", i=NEIGHBOURS)
     return dst, src
 
@@ -40,137 +43,157 @@ def tile_baum_welch_projection_s10_kernel(tc, gamma, z1_words, z1_scales, z2_wor
         psum = ctx.enter_context(tc.psum_pool(name="psum", bufs=1))
         ctx.enter_context(tc.manual_schedule())
 
-        z1s_first = keep.tile([P, R], U8, name="z1s_first", align_bytes=64)
-        z1s_rest = keep.tile([P, PASSES - 1, R], U8, name="z1s_rest", align_bytes=64)
+        z1s = [keep.tile([P, 2, R], U8, name="z1s_%d" % j, align_bytes=64) for j in range(2)]
         z2s = keep.tile([P, R], U8, name="z2s", align_bytes=64)
-        nc.vector.memset(z1s_first[:].bitcast(I32), 0)
-        nc.vector.memset(z1s_rest[:].bitcast(I32), 0)
-        nc.vector.memset(z2s[:].bitcast(I32), 0)
+        nc.gpsimd.memset(z1s[0][:].bitcast(I32), 0)
+        zeros = keep.tile([P, P * PACK], BF16, name="zeros", align_bytes=64)
+        warm_codes = keep.tile([P, P], U32, name="warm_codes", align_bytes=64)
+        warm_scales = keep.tile([P, P], U8, name="warm_scales", align_bytes=64)
+        nc.vector.memset(zeros[:], 0.0)
+        nc.gpsimd.memset(z1s[1][:].bitcast(I32), 0)
+        nc.vector.quantize_mx(out=warm_codes[:].bitcast(FP8X4), scales=warm_scales[:], in_=zeros[:])
+        warm_acc = psum.tile([P, R], F32, name="warm_acc", tag="bank%d" % (TILES - 1))
+        for n in range(WARM):
+            nc.tensor.matmul_mx(out=warm_acc[:, :P], lhsT=warm_codes[:].bitcast(FP8X4), lhsT_scale=warm_scales[:], rhs=warm_codes[:].bitcast(FP8X4), rhs_scale=warm_scales[:], start=True, stop=True)
+        nc.gpsimd.memset(z2s[:].bitcast(I32), 0)
 
         raw = {}
         z1w = {}
+        chunks = []
 
-        def load_chunk(key):
-            kind, g, h = key
+        def load_chunk(kind, g, c0, width):
+            key = (kind, g, c0, width)
             src = gamma if kind == "gamma" else z3
-            rows = src[g * K_PASS : (g + 1) * K_PASS, h * CHUNK : (h + 1) * CHUNK]
-            raw[key] = keep.tile([P, PACK, CHUNK], BF16, name="raw_%s_%d_%d" % key)
+            rows = src[g * K_PASS : (g + 1) * K_PASS, c0 : c0 + width]
+            raw[key] = keep.tile([P, PACK, width], BF16, name="raw_%s_%d_%d" % key[:3])
             nc.sync.dma_start(out=raw[key][:], in_=rows.rearrange("(p t) c -> p t c", t=PACK))
+            chunks.append(key)
 
         def load_z1_words(g):
             z1w[g] = keep.tile([P, 2 * R], U8, name="z1w_%d" % g, align_bytes=64)
             nc.sync.dma_start(out=z1w[g][:].bitcast(I32), in_=z1_words[g].bitcast(I32))
 
-        chunks = [("gamma", 0, 0), ("z3", 0, 0), ("gamma", 0, 1)]
-        for g in range(1, PASSES):
-            chunks.extend([("z3", g, 0), ("gamma", g, 0), ("gamma", g, 1)])
+        def load_z1_scales(j, queue):
+            for q in range(QUADRANTS):
+                queue.dma_start(
+                    out=z1s[j][32 * q : 32 * q + 4, :, :].bitcast(I32),
+                    in_=z1_scales[2 * j : 2 * j + 2, 4 * q : 4 * q + 4, :].rearrange("g r n -> r g n").bitcast(I32),
+                )
 
-        load_chunk(chunks[0])
-        for q in range(QUADRANTS):
-            nc.sync.dma_start(out=z1s_first[32 * q : 32 * q + 4, :].bitcast(I32), in_=z1_scales[0, 4 * q : 4 * q + 4, :].bitcast(I32))
+        load_chunk("gamma", 0, 0, NARROW)
+        load_z1_scales(0, nc.scalar)
+        load_chunk("gamma", 0, NARROW, NARROW)
         load_z1_words(0)
-        load_chunk(chunks[1])
-        load_chunk(chunks[2])
-        for q in range(QUADRANTS):
-            nc.sync.dma_start(
-                out=z1s_rest[32 * q : 32 * q + 4, :, :].bitcast(I32),
-                in_=z1_scales[1:, 4 * q : 4 * q + 4, :].rearrange("g r n -> r g n").bitcast(I32),
-            )
-        for g in range(1, PASSES):
-            load_chunk(chunks[3 * g])
-            load_z1_words(g)
-            load_chunk(chunks[3 * g + 1])
-            load_chunk(chunks[3 * g + 2])
+        for g in range(PASSES):
+            if g > 0:
+                load_chunk("gamma", g, 0, WIDE)
+                load_z1_words(g)
+            load_chunk("z3", g, 0, NARROW)
+            load_chunk("z3", g, NARROW, NARROW)
+            if g > 0:
+                load_chunk("gamma", g, WIDE, WIDE)
+            else:
+                load_chunk("gamma", g, WIDE, NARROW)
+                load_chunk("gamma", g, WIDE + NARROW, NARROW)
+            if g == 1:
+                load_z1_scales(1, nc.sync)
 
-        load_tiles = []
+        loading = {}
 
-        def load_loadings(h):
-            rows = loadings[h * CHUNK : (h + 1) * CHUNK, :]
-            tile = keep.tile([P, TILES // 2, R], BF16, name="loadings_%d" % h)
+        def load_loadings(m0, count):
+            rows = loadings[m0 * P : (m0 + count) * P, :]
+            tile = keep.tile([P, count, R], BF16, name="loadings_%d" % m0)
             nc.sync.dma_start(out=tile[:], in_=rows.rearrange("(m p) r -> p m r", p=P))
-            load_tiles.append(tile)
+            for j in range(count):
+                loading[m0 + j] = tile[:, j, :]
 
-        load_loadings(0)
+        load_loadings(0, 2)
         for q in range(QUADRANTS):
             nc.sync.dma_start(out=z2s[32 * q : 32 * q + 16, :].bitcast(I32), in_=z2_scales[:, 4 * q : 4 * q + 4, :].bitcast(I32))
-        z2w = keep.tile([P, PASSES, R], U32, name="z2w", align_bytes=64)
-        nc.sync.dma_start(out=z2w[:].bitcast(I32), in_=z2_words.rearrange("g p n t -> p g (n t)").bitcast(I32))
-        load_loadings(1)
+        z2w = []
+        for j in range(2):
+            tile = keep.tile([P, 2, R], U32, name="z2w_%d" % j, align_bytes=64)
+            nc.sync.dma_start(out=tile[:].bitcast(I32), in_=z2_words[2 * j : 2 * j + 2].rearrange("g p n t -> p g (n t)").bitcast(I32))
+            z2w.extend([tile[:, 0, :], tile[:, 1, :]])
+        load_loadings(2, 2)
+        load_loadings(4, 4)
 
         codes = {}
         scales = {}
+        for g in range(PASSES):
+            for kind, width in (("gamma", C), ("z3", R)):
+                codes[kind, g] = keep.tile([P, width], U32, name="codes_%s_%d" % (kind, g), align_bytes=64)
+                scales[kind, g] = keep.tile([P, width], U8, name="scales_%s_%d" % (kind, g), align_bytes=64)
 
-        def quantize(key, grouped, c0, width):
+        def quantize(kind, g, c0, width, grouped):
             nc.vector.quantize_mx(
-                out=codes[key][:, c0 : c0 + width].bitcast(FP8X4),
-                scales=scales[key][:, c0 : c0 + width],
+                out=codes[kind, g][:, c0 : c0 + width].bitcast(FP8X4),
+                scales=scales[kind, g][:, c0 : c0 + width],
                 in_=grouped[:],
             )
 
-        pending = None
+        pending = []
         for key in chunks:
-            codes[key] = keep.tile([P, CHUNK], U32, name="codes_%s_%d_%d" % key, align_bytes=64)
-            scales[key] = keep.tile([P, CHUNK], U8, name="scales_%s_%d_%d" % key, align_bytes=64)
-            by_scalar = keep.tile([P, HALF * PACK], BF16, name="gs_%s_%d_%d" % key, align_bytes=64)
-            dst, src = interleave_views(by_scalar, raw[key], HALF, HALF)
-            nc.scalar.copy(out=dst, in_=src)
-            if pending is not None:
-                quantize(*pending)
-            by_vector = []
-            for j in range(2):
-                grouped = keep.tile([P, QUARTER * PACK], BF16, name="gv%d_%s_%d_%d" % ((j,) + key), align_bytes=64)
-                dst, src = interleave_views(grouped, raw[key], j * QUARTER, QUARTER)
+            kind, g, chunk_c0, width = key
+            for offset in range(0, width, NARROW):
+                c0 = chunk_c0 + offset
+                grouped = keep.tile([P, NARROW * PACK], BF16, name="grouped_%s_%d_%d" % (kind, g, c0), align_bytes=64)
+                dst, src = interleave_views(grouped[:, VECTOR_COLS * PACK :], raw[key], offset + VECTOR_COLS, NARROW - VECTOR_COLS)
+                nc.scalar.copy(out=dst, in_=src)
+                dst, src = interleave_views(grouped[:, : VECTOR_COLS * PACK], raw[key], offset, VECTOR_COLS)
                 nc.vector.tensor_copy(out=dst, in_=src)
-                by_vector.append(grouped)
-            for j in range(2):
-                quantize(key, by_vector[j], j * QUARTER, QUARTER)
-            pending = (key, by_scalar, HALF, HALF)
-        quantize(*pending)
+                for job in pending:
+                    quantize(*job)
+                pending = [(kind, g, c0, NARROW, grouped)]
+                if kind == "z3" and c0 + NARROW == R:
+                    quantize(*pending[0])
+                    pending = []
+        quantize(*pending[0])
 
         def posteriors(m, g):
-            key = ("gamma", g, m // 4)
-            cols = slice((m % 4) * P, (m % 4 + 1) * P)
-            return codes[key][:, cols].bitcast(FP8X4), scales[key][:, cols]
+            cols = slice(m * P, (m + 1) * P)
+            return codes["gamma", g][:, cols].bitcast(FP8X4), scales["gamma", g][:, cols]
 
         b_acc = [psum.tile([P, R], F32, name="b_acc_%d" % m, tag="bank%d" % m) for m in range(TILES)]
 
-        def z1_pass(m, g, start, stop):
+        def z1_pass(m, g):
             lhsT, lhsT_scale = posteriors(m, g)
-            plane = z1s_first[:] if g == 0 else z1s_rest[:, g - 1, :]
-            nc.tensor.matmul_mx(out=b_acc[m][:], lhsT=lhsT, lhsT_scale=lhsT_scale, rhs=z1w[g][:].bitcast(FP4X4), rhs_scale=plane, start=start, stop=stop)
+            nc.tensor.matmul_mx(out=b_acc[m][:], lhsT=lhsT, lhsT_scale=lhsT_scale, rhs=z1w[g][:].bitcast(FP4X4), rhs_scale=z1s[g // 2][:, g % 2, :], start=(g == 0), stop=False)
 
-        def z3_pass(m, g, start, stop):
+        def z3_pass(m, g):
             lhsT, lhsT_scale = posteriors(m, g)
-            key = ("z3", g, 0)
-            nc.tensor.matmul_mx(out=b_acc[m][:], lhsT=lhsT, lhsT_scale=lhsT_scale, rhs=codes[key][:].bitcast(FP8X4), rhs_scale=scales[key][:], start=start, stop=stop)
+            nc.tensor.matmul_mx(out=b_acc[m][:], lhsT=lhsT, lhsT_scale=lhsT_scale, rhs=codes["z3", g][:].bitcast(FP8X4), rhs_scale=scales["z3", g][:], start=False, stop=(g == PASSES - 1))
 
-        for m in range(TILES // 2):
-            z1_pass(m, 0, True, False)
-        for m in range(TILES // 2):
-            z3_pass(m, 0, False, False)
-        for m in range(TILES // 2, TILES):
-            z1_pass(m, 0, True, False)
-            z3_pass(m, 0, False, False)
-        for g in range(1, PASSES):
-            for m in range(TILES):
-                z1_pass(m, g, False, False)
-                z3_pass(m, g, False, g == PASSES - 1)
+        for g in range(PASSES):
+            for m in range(EARLY_TILES):
+                z1_pass(m, g)
+            for m in range(EARLY_TILES):
+                z3_pass(m, g)
+            for m in range(EARLY_TILES, TILES):
+                z1_pass(m, g)
+                z3_pass(m, g)
 
-        loaded = []
-        for m in range(TILES):
-            tile = keep.tile([P, R], F32, name="loaded_%d" % m)
-            nc.vector.tensor_tensor(out=tile[:], in0=b_acc[m][:], in1=load_tiles[m // 4][:, m % 4, :], op=MULT)
-            loaded.append(tile)
+        loaded = {}
 
-        pieces = [(m, 0, R) for m in range(TILES - 1)] + [(TILES - 1, 0, HALF), (TILES - 1, HALF, HALF)]
+        def weigh(m):
+            loaded[m] = keep.tile([P, R], F32, name="loaded_%d" % m)
+            nc.vector.tensor_tensor(out=loaded[m][:], in0=b_acc[m][:], in1=loading[m], op=MULT)
+
+        for m in range(LEAD):
+            weigh(m)
+
+        last = TILES - 1
+        pieces = [(m, 0, R) for m in range(last - 1)] + [(last - 1, 0, 256), (last - 1, 256, 256), (last, 0, 256), (last, 256, 128), (last, 384, 128)]
         for n, (m, c0, width) in enumerate(pieces):
             cols = slice(c0, c0 + width)
+            if n + LEAD < TILES:
+                weigh(n + LEAD)
             a_acc = psum.tile([P, R], F32, name="a_acc_%d" % n, tag="bank%d" % (n % TILES))
             for g in range(PASSES):
                 lhsT, lhsT_scale = posteriors(m, g)
                 nc.tensor.matmul_mx(
                     out=a_acc[:, :width], lhsT=lhsT, lhsT_scale=lhsT_scale,
-                    rhs=z2w[:, g, cols].bitcast(FP8X4), rhs_scale=z2s[4 * g :, cols],
+                    rhs=z2w[g][:, cols].bitcast(FP8X4), rhs_scale=z2s[4 * g :, cols],
                     start=(g == 0), stop=(g == PASSES - 1),
                 )
             shrink = keep.tile([P, width], F32, name="shrink_%d" % n)

@@ -26,8 +26,8 @@ NEIGHBOURS = 4
 QUADRANTS = 4
 EARLY_TILES = 4
 LEAD = 4
-VECTOR_COLS = 112
-WARM = 16
+VECTOR_COLS = 120
+WARM = 0
 
 
 def interleave_views(grouped, raw, c0, width):
@@ -43,18 +43,10 @@ def tile_baum_welch_projection_s10_kernel(tc, gamma, z1_words, z1_scales, z2_wor
         psum = ctx.enter_context(tc.psum_pool(name="psum", bufs=1))
         ctx.enter_context(tc.manual_schedule())
 
-        z1s = [keep.tile([P, 2, R], U8, name="z1s_%d" % j, align_bytes=64) for j in range(2)]
+        z1s = keep.tile([P, PASSES, R], U8, name="z1s", align_bytes=64)
         z2s = keep.tile([P, R], U8, name="z2s", align_bytes=64)
-        nc.gpsimd.memset(z1s[0][:].bitcast(I32), 0)
-        zeros = keep.tile([P, P * PACK], BF16, name="zeros", align_bytes=64)
-        warm_codes = keep.tile([P, P], U32, name="warm_codes", align_bytes=64)
-        warm_scales = keep.tile([P, P], U8, name="warm_scales", align_bytes=64)
-        nc.vector.memset(zeros[:], 0.0)
-        nc.gpsimd.memset(z1s[1][:].bitcast(I32), 0)
-        nc.vector.quantize_mx(out=warm_codes[:].bitcast(FP8X4), scales=warm_scales[:], in_=zeros[:])
-        warm_acc = psum.tile([P, R], F32, name="warm_acc", tag="bank%d" % (TILES - 1))
-        for n in range(WARM):
-            nc.tensor.matmul_mx(out=warm_acc[:, :P], lhsT=warm_codes[:].bitcast(FP8X4), lhsT_scale=warm_scales[:], rhs=warm_codes[:].bitcast(FP8X4), rhs_scale=warm_scales[:], start=True, stop=True)
+        nc.vector.memset(z1s[:, : PASSES // 2, :].bitcast(I32), 0)
+        nc.gpsimd.memset(z1s[:, PASSES // 2 :, :].bitcast(I32), 0)
         nc.gpsimd.memset(z2s[:].bitcast(I32), 0)
 
         raw = {}
@@ -73,30 +65,18 @@ def tile_baum_welch_projection_s10_kernel(tc, gamma, z1_words, z1_scales, z2_wor
             z1w[g] = keep.tile([P, 2 * R], U8, name="z1w_%d" % g, align_bytes=64)
             nc.sync.dma_start(out=z1w[g][:].bitcast(I32), in_=z1_words[g].bitcast(I32))
 
-        def load_z1_scales(j, queue):
-            for q in range(QUADRANTS):
-                queue.dma_start(
-                    out=z1s[j][32 * q : 32 * q + 4, :, :].bitcast(I32),
-                    in_=z1_scales[2 * j : 2 * j + 2, 4 * q : 4 * q + 4, :].rearrange("g r n -> r g n").bitcast(I32),
-                )
-
-        load_chunk("gamma", 0, 0, NARROW)
-        load_z1_scales(0, nc.scalar)
-        load_chunk("gamma", 0, NARROW, NARROW)
-        load_z1_words(0)
+        load_chunk("gamma", 0, 0, WIDE)
+        for q in range(QUADRANTS):
+            nc.sync.dma_start(
+                out=z1s[32 * q : 32 * q + 4, :, :].bitcast(I32),
+                in_=z1_scales[:, 4 * q : 4 * q + 4, :].rearrange("g r n -> r g n").bitcast(I32),
+            )
         for g in range(PASSES):
             if g > 0:
                 load_chunk("gamma", g, 0, WIDE)
-                load_z1_words(g)
-            load_chunk("z3", g, 0, NARROW)
-            load_chunk("z3", g, NARROW, NARROW)
-            if g > 0:
-                load_chunk("gamma", g, WIDE, WIDE)
-            else:
-                load_chunk("gamma", g, WIDE, NARROW)
-                load_chunk("gamma", g, WIDE + NARROW, NARROW)
-            if g == 1:
-                load_z1_scales(1, nc.sync)
+            load_z1_words(g)
+            load_chunk("z3", g, 0, WIDE)
+            load_chunk("gamma", g, WIDE, WIDE)
 
         loading = {}
 
@@ -111,10 +91,10 @@ def tile_baum_welch_projection_s10_kernel(tc, gamma, z1_words, z1_scales, z2_wor
         for q in range(QUADRANTS):
             nc.sync.dma_start(out=z2s[32 * q : 32 * q + 16, :].bitcast(I32), in_=z2_scales[:, 4 * q : 4 * q + 4, :].bitcast(I32))
         z2w = []
-        for j in range(2):
-            tile = keep.tile([P, 2, R], U32, name="z2w_%d" % j, align_bytes=64)
-            nc.sync.dma_start(out=tile[:].bitcast(I32), in_=z2_words[2 * j : 2 * j + 2].rearrange("g p n t -> p g (n t)").bitcast(I32))
-            z2w.extend([tile[:, 0, :], tile[:, 1, :]])
+        for g in range(PASSES):
+            tile = keep.tile([P, R], U32, name="z2w_%d" % g, align_bytes=64)
+            nc.sync.dma_start(out=tile[:].bitcast(I32), in_=z2_words[g].rearrange("p n t -> p (n t)").bitcast(I32))
+            z2w.append(tile)
         load_loadings(2, 2)
         load_loadings(4, 4)
 
@@ -132,9 +112,9 @@ def tile_baum_welch_projection_s10_kernel(tc, gamma, z1_words, z1_scales, z2_wor
                 in_=grouped[:],
             )
 
-        pending = []
         for key in chunks:
             kind, g, chunk_c0, width = key
+            jobs = []
             for offset in range(0, width, NARROW):
                 c0 = chunk_c0 + offset
                 grouped = keep.tile([P, NARROW * PACK], BF16, name="grouped_%s_%d_%d" % (kind, g, c0), align_bytes=64)
@@ -142,13 +122,9 @@ def tile_baum_welch_projection_s10_kernel(tc, gamma, z1_words, z1_scales, z2_wor
                 nc.scalar.copy(out=dst, in_=src)
                 dst, src = interleave_views(grouped[:, : VECTOR_COLS * PACK], raw[key], offset, VECTOR_COLS)
                 nc.vector.tensor_copy(out=dst, in_=src)
-                for job in pending:
-                    quantize(*job)
-                pending = [(kind, g, c0, NARROW, grouped)]
-                if kind == "z3" and c0 + NARROW == R:
-                    quantize(*pending[0])
-                    pending = []
-        quantize(*pending[0])
+                jobs.append((kind, g, c0, NARROW, grouped))
+            for job in jobs:
+                quantize(*job)
 
         def posteriors(m, g):
             cols = slice(m * P, (m + 1) * P)
@@ -158,7 +134,7 @@ def tile_baum_welch_projection_s10_kernel(tc, gamma, z1_words, z1_scales, z2_wor
 
         def z1_pass(m, g):
             lhsT, lhsT_scale = posteriors(m, g)
-            nc.tensor.matmul_mx(out=b_acc[m][:], lhsT=lhsT, lhsT_scale=lhsT_scale, rhs=z1w[g][:].bitcast(FP4X4), rhs_scale=z1s[g // 2][:, g % 2, :], start=(g == 0), stop=False)
+            nc.tensor.matmul_mx(out=b_acc[m][:], lhsT=lhsT, lhsT_scale=lhsT_scale, rhs=z1w[g][:].bitcast(FP4X4), rhs_scale=z1s[:, g, :], start=(g == 0), stop=False)
 
         def z3_pass(m, g):
             lhsT, lhsT_scale = posteriors(m, g)

@@ -18,20 +18,20 @@ SIGMOID = mybir.ActivationFunctionType.Sigmoid
 P = 128
 PACK = 4
 K_PASS = P * PACK
-PASSES = T // K_PASS
+GROUPS = T // K_PASS
 TILES = C // P
-WIDE = 512
-NARROW = 256
+QUADRANT = 32
+SCALE_ROWS = 4
+CHUNK = 512
+CHUNK_TILES = CHUNK // P
+HALF = CHUNK // 2
+QUARTER = CHUNK // 4
 NEIGHBOURS = 4
-QUADRANTS = 4
-EARLY_TILES = 4
 LEAD = 4
-VECTOR_COLS = 120
-WARM = 0
 
 
 def interleave_views(grouped, raw, c0, width):
-    dst = grouped.rearrange("p (c i t) -> p c t i", i=NEIGHBOURS, t=PACK)
+    dst = grouped[:].rearrange("p (c i t) -> p c t i", i=NEIGHBOURS, t=PACK)
     src = raw[:, :, c0 : c0 + width].rearrange("p t (c i) -> p c t i", i=NEIGHBOURS)
     return dst, src
 
@@ -43,40 +43,53 @@ def tile_baum_welch_projection_s10_kernel(tc, gamma, z1_words, z1_scales, z2_wor
         psum = ctx.enter_context(tc.psum_pool(name="psum", bufs=1))
         ctx.enter_context(tc.manual_schedule())
 
-        z1s = keep.tile([P, PASSES, R], U8, name="z1s", align_bytes=64)
-        z2s = keep.tile([P, R], U8, name="z2s", align_bytes=64)
-        nc.vector.memset(z1s[:, : PASSES // 2, :].bitcast(I32), 0)
-        nc.gpsimd.memset(z1s[:, PASSES // 2 :, :].bitcast(I32), 0)
-        nc.gpsimd.memset(z2s[:].bitcast(I32), 0)
+        z1_plane_first = keep.tile([P, R], U8, name="z1_plane_first", align_bytes=64)
+        z1_planes_rest = keep.tile([P, GROUPS - 1, R], U8, name="z1_planes_rest", align_bytes=64)
+        z2_planes = keep.tile([P, R], U8, name="z2_planes", align_bytes=64)
+        nc.vector.memset(z1_plane_first[:].bitcast(I32), 0)
+        nc.vector.memset(z1_planes_rest[:].bitcast(I32), 0)
+        nc.vector.memset(z2_planes[:].bitcast(I32), 0)
 
         raw = {}
-        z1w = {}
-        chunks = []
+        z1_codes = {}
 
-        def load_chunk(kind, g, c0, width):
-            key = (kind, g, c0, width)
-            src = gamma if kind == "gamma" else z3
-            rows = src[g * K_PASS : (g + 1) * K_PASS, c0 : c0 + width]
-            raw[key] = keep.tile([P, PACK, width], BF16, name="raw_%s_%d_%d" % key[:3])
-            nc.sync.dma_start(out=raw[key][:], in_=rows.rearrange("(p t) c -> p t c", t=PACK))
-            chunks.append(key)
+        def load_chunk(chunk):
+            kind, g, h = chunk
+            source = gamma if kind == "gamma" else z3
+            rows = source[g * K_PASS : (g + 1) * K_PASS, h * CHUNK : (h + 1) * CHUNK]
+            raw[chunk] = keep.tile([P, PACK, CHUNK], BF16, name="raw_%s_%d_%d" % chunk)
+            nc.sync.dma_start(out=raw[chunk][:], in_=rows.rearrange("(p t) c -> p t c", t=PACK))
 
         def load_z1_words(g):
-            z1w[g] = keep.tile([P, 2 * R], U8, name="z1w_%d" % g, align_bytes=64)
-            nc.sync.dma_start(out=z1w[g][:].bitcast(I32), in_=z1_words[g].bitcast(I32))
+            z1_codes[g] = keep.tile([P, 2 * R], U8, name="z1_codes_%d" % g, align_bytes=64)
+            nc.sync.dma_start(out=z1_codes[g][:].bitcast(I32), in_=z1_words[g].bitcast(I32))
 
-        load_chunk("gamma", 0, 0, WIDE)
-        for q in range(QUADRANTS):
+        def scale_rows(q):
+            return slice(SCALE_ROWS * q, SCALE_ROWS * (q + 1))
+
+        chunks = []
+        for g in range(GROUPS):
+            chunks.extend([("gamma", g, 0), ("z3", g, 0), ("gamma", g, 1)])
+
+        load_chunk(chunks[0])
+        for q in range(P // QUADRANT):
             nc.sync.dma_start(
-                out=z1s[32 * q : 32 * q + 4, :, :].bitcast(I32),
-                in_=z1_scales[:, 4 * q : 4 * q + 4, :].rearrange("g r n -> r g n").bitcast(I32),
+                out=z1_plane_first[QUADRANT * q : QUADRANT * q + SCALE_ROWS, :].bitcast(I32),
+                in_=z1_scales[0, scale_rows(q), :].bitcast(I32),
             )
-        for g in range(PASSES):
-            if g > 0:
-                load_chunk("gamma", g, 0, WIDE)
+        load_z1_words(0)
+        load_chunk(chunks[1])
+        load_chunk(chunks[2])
+        for q in range(P // QUADRANT):
+            nc.sync.dma_start(
+                out=z1_planes_rest[QUADRANT * q : QUADRANT * q + SCALE_ROWS, :, :].bitcast(I32),
+                in_=z1_scales[1:, scale_rows(q), :].rearrange("g r n -> r g n").bitcast(I32),
+            )
+        for g in range(1, GROUPS):
+            load_chunk(chunks[3 * g])
             load_z1_words(g)
-            load_chunk("z3", g, 0, WIDE)
-            load_chunk("gamma", g, WIDE, WIDE)
+            load_chunk(chunks[3 * g + 1])
+            load_chunk(chunks[3 * g + 2])
 
         loading = {}
 
@@ -88,92 +101,110 @@ def tile_baum_welch_projection_s10_kernel(tc, gamma, z1_words, z1_scales, z2_wor
                 loading[m0 + j] = tile[:, j, :]
 
         load_loadings(0, 2)
-        for q in range(QUADRANTS):
-            nc.sync.dma_start(out=z2s[32 * q : 32 * q + 16, :].bitcast(I32), in_=z2_scales[:, 4 * q : 4 * q + 4, :].bitcast(I32))
-        z2w = []
-        for g in range(PASSES):
-            tile = keep.tile([P, R], U32, name="z2w_%d" % g, align_bytes=64)
+        for q in range(P // QUADRANT):
+            nc.sync.dma_start(
+                out=z2_planes[QUADRANT * q : QUADRANT * q + GROUPS * SCALE_ROWS, :].bitcast(I32),
+                in_=z2_scales[:, scale_rows(q), :].bitcast(I32),
+            )
+        z2_codes = []
+        for g in range(GROUPS):
+            tile = keep.tile([P, R], U32, name="z2_codes_%d" % g, align_bytes=64)
             nc.sync.dma_start(out=tile[:].bitcast(I32), in_=z2_words[g].rearrange("p n t -> p (n t)").bitcast(I32))
-            z2w.append(tile)
+            z2_codes.append(tile)
         load_loadings(2, 2)
         load_loadings(4, 4)
 
         codes = {}
-        scales = {}
-        for g in range(PASSES):
-            for kind, width in (("gamma", C), ("z3", R)):
-                codes[kind, g] = keep.tile([P, width], U32, name="codes_%s_%d" % (kind, g), align_bytes=64)
-                scales[kind, g] = keep.tile([P, width], U8, name="scales_%s_%d" % (kind, g), align_bytes=64)
+        planes = {}
 
-        def quantize(kind, g, c0, width, grouped):
+        def quantize(chunk, grouped, c0, width):
             nc.vector.quantize_mx(
-                out=codes[kind, g][:, c0 : c0 + width].bitcast(FP8X4),
-                scales=scales[kind, g][:, c0 : c0 + width],
+                out=codes[chunk][:, c0 : c0 + width].bitcast(FP8X4),
+                scales=planes[chunk][:, c0 : c0 + width],
                 in_=grouped[:],
             )
 
-        for key in chunks:
-            kind, g, chunk_c0, width = key
-            jobs = []
-            for offset in range(0, width, NARROW):
-                c0 = chunk_c0 + offset
-                grouped = keep.tile([P, NARROW * PACK], BF16, name="grouped_%s_%d_%d" % (kind, g, c0), align_bytes=64)
-                dst, src = interleave_views(grouped[:, VECTOR_COLS * PACK :], raw[key], offset + VECTOR_COLS, NARROW - VECTOR_COLS)
-                nc.scalar.copy(out=dst, in_=src)
-                dst, src = interleave_views(grouped[:, : VECTOR_COLS * PACK], raw[key], offset, VECTOR_COLS)
+        scalar_job = None
+        for chunk in chunks:
+            codes[chunk] = keep.tile([P, CHUNK], U32, name="codes_%s_%d_%d" % chunk, align_bytes=64)
+            planes[chunk] = keep.tile([P, CHUNK], U8, name="plane_%s_%d_%d" % chunk, align_bytes=64)
+            by_scalar = keep.tile([P, HALF * PACK], BF16, name="by_scalar_%s_%d_%d" % chunk, align_bytes=64)
+            dst, src = interleave_views(by_scalar, raw[chunk], HALF, HALF)
+            nc.scalar.copy(out=dst, in_=src)
+            if scalar_job is not None:
+                quantize(*scalar_job)
+            by_vector = []
+            for j in range(2):
+                grouped = keep.tile([P, QUARTER * PACK], BF16, name="by_vector_%d_%s_%d_%d" % ((j,) + chunk), align_bytes=64)
+                dst, src = interleave_views(grouped, raw[chunk], j * QUARTER, QUARTER)
                 nc.vector.tensor_copy(out=dst, in_=src)
-                jobs.append((kind, g, c0, NARROW, grouped))
-            for job in jobs:
-                quantize(*job)
+                by_vector.append(grouped)
+            for j in range(2):
+                quantize(chunk, by_vector[j], j * QUARTER, QUARTER)
+            scalar_job = (chunk, by_scalar, HALF, HALF)
+        quantize(*scalar_job)
 
         def posteriors(m, g):
-            cols = slice(m * P, (m + 1) * P)
-            return codes["gamma", g][:, cols].bitcast(FP8X4), scales["gamma", g][:, cols]
+            chunk = ("gamma", g, m // CHUNK_TILES)
+            cols = slice((m % CHUNK_TILES) * P, (m % CHUNK_TILES + 1) * P)
+            return codes[chunk][:, cols].bitcast(FP8X4), planes[chunk][:, cols]
 
         b_acc = [psum.tile([P, R], F32, name="b_acc_%d" % m, tag="bank%d" % m) for m in range(TILES)]
 
         def z1_pass(m, g):
             lhsT, lhsT_scale = posteriors(m, g)
-            nc.tensor.matmul_mx(out=b_acc[m][:], lhsT=lhsT, lhsT_scale=lhsT_scale, rhs=z1w[g][:].bitcast(FP4X4), rhs_scale=z1s[:, g, :], start=(g == 0), stop=False)
+            plane = z1_plane_first[:] if g == 0 else z1_planes_rest[:, g - 1, :]
+            nc.tensor.matmul_mx(
+                out=b_acc[m][:], lhsT=lhsT, lhsT_scale=lhsT_scale,
+                rhs=z1_codes[g][:].bitcast(FP4X4), rhs_scale=plane,
+                start=(g == 0), stop=False,
+            )
 
         def z3_pass(m, g):
             lhsT, lhsT_scale = posteriors(m, g)
-            nc.tensor.matmul_mx(out=b_acc[m][:], lhsT=lhsT, lhsT_scale=lhsT_scale, rhs=codes["z3", g][:].bitcast(FP8X4), rhs_scale=scales["z3", g][:], start=False, stop=(g == PASSES - 1))
+            chunk = ("z3", g, 0)
+            nc.tensor.matmul_mx(
+                out=b_acc[m][:], lhsT=lhsT, lhsT_scale=lhsT_scale,
+                rhs=codes[chunk][:].bitcast(FP8X4), rhs_scale=planes[chunk][:],
+                start=False, stop=(g == GROUPS - 1),
+            )
 
-        for g in range(PASSES):
-            for m in range(EARLY_TILES):
+        for g in range(GROUPS):
+            for m in range(CHUNK_TILES):
                 z1_pass(m, g)
-            for m in range(EARLY_TILES):
+            for m in range(CHUNK_TILES):
                 z3_pass(m, g)
-            for m in range(EARLY_TILES, TILES):
+            for m in range(CHUNK_TILES, TILES):
                 z1_pass(m, g)
                 z3_pass(m, g)
 
-        loaded = {}
+        weighed = {}
 
         def weigh(m):
-            loaded[m] = keep.tile([P, R], F32, name="loaded_%d" % m)
-            nc.vector.tensor_tensor(out=loaded[m][:], in0=b_acc[m][:], in1=loading[m], op=MULT)
+            weighed[m] = keep.tile([P, R], F32, name="weighed_%d" % m)
+            nc.vector.tensor_tensor(out=weighed[m][:], in0=b_acc[m][:], in1=loading[m], op=MULT)
 
         for m in range(LEAD):
             weigh(m)
 
         last = TILES - 1
-        pieces = [(m, 0, R) for m in range(last - 1)] + [(last - 1, 0, 256), (last - 1, 256, 256), (last, 0, 256), (last, 256, 128), (last, 384, 128)]
+        pieces = [(m, 0, R) for m in range(last - 1)]
+        pieces.extend([(last - 1, 0, R // 2), (last - 1, R // 2, R // 2)])
+        pieces.extend([(last, 0, R // 2), (last, R // 2, R // 4), (last, 3 * R // 4, R // 4)])
         for n, (m, c0, width) in enumerate(pieces):
             cols = slice(c0, c0 + width)
             if n + LEAD < TILES:
                 weigh(n + LEAD)
             a_acc = psum.tile([P, R], F32, name="a_acc_%d" % n, tag="bank%d" % (n % TILES))
-            for g in range(PASSES):
+            for g in range(GROUPS):
                 lhsT, lhsT_scale = posteriors(m, g)
                 nc.tensor.matmul_mx(
                     out=a_acc[:, :width], lhsT=lhsT, lhsT_scale=lhsT_scale,
-                    rhs=z2w[g][:, cols].bitcast(FP8X4), rhs_scale=z2s[4 * g :, cols],
-                    start=(g == 0), stop=(g == PASSES - 1),
+                    rhs=z2_codes[g][:, cols].bitcast(FP8X4), rhs_scale=z2_planes[SCALE_ROWS * g :, cols],
+                    start=(g == 0), stop=(g == GROUPS - 1),
                 )
             shrink = keep.tile([P, width], F32, name="shrink_%d" % n)
             nc.scalar.activation(out=shrink[:], in_=a_acc[:, :width], func=SIGMOID)
             result = keep.tile([P, width], F32, name="result_%d" % n)
-            nc.vector.tensor_tensor(out=result[:], in0=shrink[:], in1=loaded[m][:, cols], op=MULT)
+            nc.vector.tensor_tensor(out=result[:], in0=shrink[:], in1=weighed[m][:, cols], op=MULT)
             nc.sync.dma_start(out=out[m * P : (m + 1) * P, cols], in_=result[:])

from contextlib import ExitStack

import concourse.mybir as mybir

T, C, R = 2048, 1024, 512
FLOPS = 3 * 2 * T * C * R

F32 = mybir.dt.float32
BF16 = mybir.dt.bfloat16
I32 = mybir.dt.int32
U32 = mybir.dt.uint32
U8 = mybir.dt.uint8
FP8X4 = mybir.dt.float8_e4m3fn_x4
FP4X4 = mybir.dt.float4_e2m1fn_x4
MULT = mybir.AluOpType.mult
SIGMOID = mybir.ActivationFunctionType.Sigmoid

P = 128
PACK = 4
K_PASS = P * PACK
GROUPS = T // K_PASS
TILES = C // P
QUADRANT = 32
SCALE_ROWS = 4
CHUNK = 512
CHUNK_TILES = CHUNK // P
HALF = CHUNK // 2
QUARTER = CHUNK // 4
NEIGHBOURS = 4
LEAD = 4


def interleave_views(grouped, raw, c0, width):
    dst = grouped[:].rearrange("p (c i t) -> p c t i", i=NEIGHBOURS, t=PACK)
    src = raw[:, :, c0 : c0 + width].rearrange("p t (c i) -> p c t i", i=NEIGHBOURS)
    return dst, src


def tile_baum_welch_projection_s10_kernel(tc, gamma, z1_words, z1_scales, z2_words, z2_scales, z3, loadings, out):
    nc = tc.nc
    with ExitStack() as ctx:
        keep = ctx.enter_context(tc.tile_pool(name="keep", bufs=1))
        psum = ctx.enter_context(tc.psum_pool(name="psum", bufs=1))
        ctx.enter_context(tc.manual_schedule())

        z1_plane_first = keep.tile([P, R], U8, name="z1_plane_first", align_bytes=64)
        z1_planes_rest = keep.tile([P, GROUPS - 1, R], U8, name="z1_planes_rest", align_bytes=64)
        z2_planes = keep.tile([P, R], U8, name="z2_planes", align_bytes=64)
        nc.vector.memset(z1_plane_first[:].bitcast(I32), 0)
        nc.vector.memset(z1_planes_rest[:].bitcast(I32), 0)
        nc.vector.memset(z2_planes[:].bitcast(I32), 0)

        raw = {}
        z1_codes = {}

        def load_chunk(chunk):
            kind, g, h = chunk
            source = gamma if kind == "gamma" else z3
            rows = source[g * K_PASS : (g + 1) * K_PASS, h * CHUNK : (h + 1) * CHUNK]
            raw[chunk] = keep.tile([P, PACK, CHUNK], BF16, name="raw_%s_%d_%d" % chunk)
            nc.sync.dma_start(out=raw[chunk][:], in_=rows.rearrange("(p t) c -> p t c", t=PACK))

        def load_z1_words(g):
            z1_codes[g] = keep.tile([P, 2 * R], U8, name="z1_codes_%d" % g, align_bytes=64)
            nc.sync.dma_start(out=z1_codes[g][:].bitcast(I32), in_=z1_words[g].bitcast(I32))

        def scale_rows(q):
            return slice(SCALE_ROWS * q, SCALE_ROWS * (q + 1))

        chunks = []
        for g in range(GROUPS):
            chunks.extend([("gamma", g, 0), ("z3", g, 0), ("gamma", g, 1)])

        load_chunk(chunks[0])
        for q in range(P // QUADRANT):
            nc.sync.dma_start(
                out=z1_plane_first[QUADRANT * q : QUADRANT * q + SCALE_ROWS, :].bitcast(I32),
                in_=z1_scales[0, scale_rows(q), :].bitcast(I32),
            )
        load_z1_words(0)
        load_chunk(chunks[1])
        load_chunk(chunks[2])
        for q in range(P // QUADRANT):
            nc.sync.dma_start(
                out=z1_planes_rest[QUADRANT * q : QUADRANT * q + SCALE_ROWS, :, :].bitcast(I32),
                in_=z1_scales[1:, scale_rows(q), :].rearrange("g r n -> r g n").bitcast(I32),
            )
        for g in range(1, GROUPS):
            load_chunk(chunks[3 * g])
            load_z1_words(g)
            load_chunk(chunks[3 * g + 1])
            load_chunk(chunks[3 * g + 2])

        loading = {}

        def load_loadings(m0, count):
            rows = loadings[m0 * P : (m0 + count) * P, :]
            tile = keep.tile([P, count, R], BF16, name="loadings_%d" % m0)
            nc.sync.dma_start(out=tile[:], in_=rows.rearrange("(m p) r -> p m r", p=P))
            for j in range(count):
                loading[m0 + j] = tile[:, j, :]

        load_loadings(0, 2)
        for q in range(P // QUADRANT):
            nc.sync.dma_start(
                out=z2_planes[QUADRANT * q : QUADRANT * q + GROUPS * SCALE_ROWS, :].bitcast(I32),
                in_=z2_scales[:, scale_rows(q), :].bitcast(I32),
            )
        z2_codes = []
        for g in range(GROUPS):
            tile = keep.tile([P, R], U32, name="z2_codes_%d" % g, align_bytes=64)
            nc.sync.dma_start(out=tile[:].bitcast(I32), in_=z2_words[g].rearrange("p n t -> p (n t)").bitcast(I32))
            z2_codes.append(tile)
        load_loadings(2, 2)
        load_loadings(4, 4)

        codes = {}
        planes = {}

        def quantize(chunk, grouped, c0, width):
            nc.vector.quantize_mx(
                out=codes[chunk][:, c0 : c0 + width].bitcast(FP8X4),
                scales=planes[chunk][:, c0 : c0 + width],
                in_=grouped[:],
            )

        scalar_job = None
        for chunk in chunks:
            codes[chunk] = keep.tile([P, CHUNK], U32, name="codes_%s_%d_%d" % chunk, align_bytes=64)
            planes[chunk] = keep.tile([P, CHUNK], U8, name="plane_%s_%d_%d" % chunk, align_bytes=64)
            by_scalar = keep.tile([P, HALF * PACK], BF16, name="by_scalar_%s_%d_%d" % chunk, align_bytes=64)
            dst, src = interleave_views(by_scalar, raw[chunk], HALF, HALF)
            nc.scalar.copy(out=dst, in_=src)
            if scalar_job is not None:
                quantize(*scalar_job)
            by_vector = []
            for j in range(2):
                grouped = keep.tile([P, QUARTER * PACK], BF16, name="by_vector_%d_%s_%d_%d" % ((j,) + chunk), align_bytes=64)
                dst, src = interleave_views(grouped, raw[chunk], j * QUARTER, QUARTER)
                nc.vector.tensor_copy(out=dst, in_=src)
                by_vector.append(grouped)
            for j in range(2):
                quantize(chunk, by_vector[j], j * QUARTER, QUARTER)
            scalar_job = (chunk, by_scalar, HALF, HALF)
        quantize(*scalar_job)

        def posteriors(m, g):
            chunk = ("gamma", g, m // CHUNK_TILES)
            cols = slice((m % CHUNK_TILES) * P, (m % CHUNK_TILES + 1) * P)
            return codes[chunk][:, cols].bitcast(FP8X4), planes[chunk][:, cols]

        b_acc = [psum.tile([P, R], F32, name="b_acc_%d" % m, tag="bank%d" % m) for m in range(TILES)]

        def z1_pass(m, g):
            lhsT, lhsT_scale = posteriors(m, g)
            plane = z1_plane_first[:] if g == 0 else z1_planes_rest[:, g - 1, :]
            nc.tensor.matmul_mx(
                out=b_acc[m][:], lhsT=lhsT, lhsT_scale=lhsT_scale,
                rhs=z1_codes[g][:].bitcast(FP4X4), rhs_scale=plane,
                start=(g == 0), stop=False,
            )

        def z3_pass(m, g):
            lhsT, lhsT_scale = posteriors(m, g)
            chunk = ("z3", g, 0)
            nc.tensor.matmul_mx(
                out=b_acc[m][:], lhsT=lhsT, lhsT_scale=lhsT_scale,
                rhs=codes[chunk][:].bitcast(FP8X4), rhs_scale=planes[chunk][:],
                start=False, stop=(g == GROUPS - 1),
            )

        for g in range(GROUPS):
            for m in range(CHUNK_TILES):
                z1_pass(m, g)
            for m in range(CHUNK_TILES):
                z3_pass(m, g)
            for m in range(CHUNK_TILES, TILES):
                z1_pass(m, g)
                z3_pass(m, g)

        weighed = {}

        def weigh(m):
            weighed[m] = keep.tile([P, R], F32, name="weighed_%d" % m)
            nc.vector.tensor_tensor(out=weighed[m][:], in0=b_acc[m][:], in1=loading[m], op=MULT)

        for m in range(LEAD):
            weigh(m)

        last = TILES - 1
        pieces = [(m, 0, R) for m in range(last - 1)]
        pieces.extend([(last - 1, 0, R // 2), (last - 1, R // 2, R // 2)])
        pieces.extend([(last, 0, R // 2), (last, R // 2, R // 4), (last, 3 * R // 4, R // 4)])
        for n, (m, c0, width) in enumerate(pieces):
            cols = slice(c0, c0 + width)
            if n + LEAD < TILES:
                weigh(n + LEAD)
            a_acc = psum.tile([P, R], F32, name="a_acc_%d" % n, tag="bank%d" % (n % TILES))
            for g in range(GROUPS):
                lhsT, lhsT_scale = posteriors(m, g)
                nc.tensor.matmul_mx(
                    out=a_acc[:, :width], lhsT=lhsT, lhsT_scale=lhsT_scale,
                    rhs=z2_codes[g][:, cols].bitcast(FP8X4), rhs_scale=z2_planes[SCALE_ROWS * g :, cols],
                    start=(g == 0), stop=(g == GROUPS - 1),
                )
            shrink = keep.tile([P, width], F32, name="shrink_%d" % n)
            nc.scalar.activation(out=shrink[:], in_=a_acc[:, :width], func=SIGMOID)
            result = keep.tile([P, width], F32, name="result_%d" % n)
            nc.vector.tensor_tensor(out=result[:], in0=shrink[:], in1=weighed[m][:, cols], op=MULT)
            nc.sync.dma_start(out=out[m * P : (m + 1) * P, cols], in_=result[:])
